import numpy as np
import ml_dtypes


def mxq(x, axis, fmt="e4m3"):
    dtype, down = {"e4m3": (ml_dtypes.float8_e4m3fn, 7), "e5m2": (ml_dtypes.float8_e5m2, 14)}[fmt]
    v = np.moveaxis(np.asarray(x, np.float32).astype(ml_dtypes.bfloat16).astype(np.float64), axis, -1)
    blocks = v.reshape(v.shape[:-1] + (-1, 32))
    amax = np.abs(blocks).max(-1, keepdims=True)
    byte = np.maximum(np.where(amax > 0, np.frexp(amax)[1] - 1 + 127, 0) - down, 1)
    scale = np.exp2(byte - 127.0)
    codes = (blocks / scale).astype(np.float32).astype(dtype).astype(np.float64)
    return np.moveaxis((codes * scale).reshape(v.shape), -1, axis)


WIDE = False


def mx_kscale(k):
    if not WIDE:
        return np.ones(k)
    levels = np.array([10, -10, 5, -5, 0])
    if k % 512:
        return np.exp2(np.random.permutation(np.resize(levels, k // 32))).repeat(32)
    a = np.empty((k // 512, 16))
    for p in range(k // 512):
        a[p, :8] = np.random.permutation(np.resize(levels, 8))
        for g in range(8):
            far = levels[np.abs(levels - a[p, g]) >= 10]
            a[p, g + 8] = far[np.random.randint(len(far))]
    return np.exp2(a.ravel()).repeat(32)


def f64(x):
    return np.asarray(x).astype(np.float64)


def striped(idx):
    return np.tile(idx.reshape(-1, 16).T, (8, 1)).astype(np.uint16)


def unstriped(offs):
    return offs[:16].T.reshape(-1).astype(np.int64)


E2M1 = np.array([0.0, 0.5, 1.0, 1.5, 2.0, 3.0, 4.0, 6.0, -0.0, -0.5, -1.0, -1.5, -2.0, -3.0, -4.0, -6.0])


def pack_weight(w, fmt):
    k, n = w.shape
    w = f64(np.asarray(w, np.float32).astype(ml_dtypes.bfloat16)).reshape(k // 32, 32, n)
    amax = np.abs(w).max(1)
    if fmt == "e4m3":
        byte = np.frexp(amax)[1] - 1 + 127 - 7
    else:
        mant, ex = np.frexp(amax / 6.0)
        byte = np.where(mant > 0.5, ex, ex - 1) + 127
    byte = np.clip(np.where(amax > 0, byte, 1), 1, 254)
    scaled = (w * np.exp2(127.0 - byte)[:, None, :]).reshape(k, n).astype(np.float32)
    by_word = np.ascontiguousarray(scaled.reshape(k // 512, 128, 4, n).transpose(0, 1, 3, 2))
    if fmt == "e4m3":
        words = by_word.astype(ml_dtypes.float8_e4m3fn).view(np.uint8)
    else:
        c = by_word.astype(ml_dtypes.float4_e2m1fn).view(np.uint8) & 0xF
        words = (c[..., 0::2] | (c[..., 1::2] << 4)).reshape(k // 512, 128, 2 * n)
    return np.ascontiguousarray(words), np.ascontiguousarray(byte.astype(np.uint8).reshape(k // 512, 16, n))


def unpack_weight(words, scales, fmt):
    g, _, n = scales.shape
    words = np.ascontiguousarray(words).reshape(g, 128, n, -1)
    if fmt == "e4m3":
        vals = words.view(ml_dtypes.float8_e4m3fn).astype(np.float64)
    else:
        nib = np.empty((g, 128, n, 4), np.uint8)
        nib[..., 0::2] = words & 0xF
        nib[..., 1::2] = words >> 4
        vals = E2M1[nib]
    vals = vals * np.repeat(np.exp2(scales.astype(np.float64) - 127.0), 8, axis=1)[..., None]
    return vals.transpose(0, 1, 3, 2).reshape(g * 512, n)


def planes(y):
    n, m = y.shape
    v = y.astype(np.float32).astype(ml_dtypes.bfloat16).astype(np.float64).reshape(n // 32, 32, m)
    top = np.abs(v).max(1)
    byte = np.clip(np.where(top > 0, np.frexp(top)[1] - 1 + 127 - 7, 1), 1, 254)
    codes = (v * np.exp2(127.0 - byte)[:, None, :]).reshape(n, m).astype(np.float32).astype(ml_dtypes.float8_e4m3fn).view(np.uint8)
    words = codes.reshape(n // 512, 128, 4, m).transpose(0, 1, 3, 2)
    return np.ascontiguousarray(words), np.ascontiguousarray(byte.astype(np.uint8).reshape(n // 512, 16, m))


def relu2(v):
    return np.maximum(v, 0.0) ** 2


def silu(v):
    return v / (1.0 + np.exp(-np.maximum(v, -700.0)))


K, T, E, C, H, N = 512, 512, 4, 256, 512, 512


def by_expert(wq, xq):
    return np.concatenate([wq[e].T @ xq[:, e * C:(e + 1) * C] for e in range(E)], axis=1)


def setup_inputs():
    n = np.random.standard_normal
    s = mx_kscale(K)
    u = mx_kscale(H)
    first = np.random.permutation(np.repeat(np.arange(E), T // E))
    second = (first + 1 + np.random.permutation(np.repeat(np.arange(E - 1), -(-T // (E - 1)))[:T])) % E
    while np.bincount(second, minlength=E).max() != T // E:
        load = np.bincount(second, minlength=E); hi, lo = int(load.argmax()), int(load.argmin())
        t = np.flatnonzero((second == hi) & (first != lo))[0]; second[t] = lo
    slot_token = np.empty(E * C, np.int64); pos = np.empty((2, T), np.int64); fill = np.zeros(E, np.int64)
    place = np.stack([np.random.permutation(C) for _ in range(E)])
    for r, deal in enumerate((first, second)):
        for t in np.random.permutation(T):
            e = deal[t]; j = e * C + place[e, fill[e]]; fill[e] += 1; slot_token[j] = t; pos[r, t] = j
    g = np.random.uniform(0.2, 0.8, T)
    x = pack_weight(n((K, T)) * s[:, None], "e4m3")
    wg = pack_weight(n((K, N)) / np.sqrt(K) / s[:, None], "e2m1")
    w1 = [pack_weight(m, "e4m3") for m in n((E, K, H)) / np.sqrt(K) / s[None, :, None] * u]
    w2 = [pack_weight(m, "e4m3") for m in n((E, H, N)) / np.sqrt(H) / u[None, :, None] ** 2]
    return {
        "x_words": x[0],
        "x_scales": x[1],
        "wg_words": wg[0],
        "wg_scales": wg[1],
        "w1_words": np.stack([m[0] for m in w1]),
        "w1_scales": np.stack([m[1] for m in w1]),
        "w2_words": np.stack([m[0] for m in w2]),
        "w2_scales": np.stack([m[1] for m in w2]),
        "gate": np.stack([np.tile(g, (128, 1)), np.tile(1.0 - g, (128, 1))]).astype(np.float32),
        "offs": striped(slot_token),
        "pos1": striped(pos[0]),
        "pos2": striped(pos[1]),
    }


def reference(x_words, x_scales, wg_words, wg_scales, w1_words, w1_scales, w2_words, w2_scales, gate, offs, pos1, pos2):
    wg = unpack_weight(wg_words, wg_scales, "e2m1")
    w1 = np.stack([unpack_weight(w1_words[e], w1_scales[e], "e4m3") for e in range(E)])
    w2 = np.stack([unpack_weight(w2_words[e], w2_scales[e], "e4m3") for e in range(E)])
    idx = unstriped(offs)
    x = unpack_weight(x_words, x_scales, "e4m3")
    o = silu(wg.T @ x)
    h = relu2(by_expert(w1, x[:, idx]))
    y = by_expert(w2, mxq(h, 0, "e4m3"))
    c = sum(f64(gate[r, :1]) * y[:, unstriped(p)] for r, p in enumerate((pos1, pos2)))
    out_0 = o * c
    return (out_0,) + planes(out_0)

@@ -1,0 +1,192 @@
+from contextlib import ExitStack
+
+import concourse.mybir as mybir
+
+K, T, E, C, H, N = 512, 512, 4, 256, 512, 512
+S = E * C
+FLOPS = 2 * K * N * T + 2 * K * H * S + 2 * H * N * S
+
+F32 = mybir.dt.float32
+BF16 = mybir.dt.bfloat16
+I32 = mybir.dt.int32
+U32 = mybir.dt.uint32
+U16 = mybir.dt.uint16
+U8 = mybir.dt.uint8
+FP8X4 = mybir.dt.float8_e4m3fn_x4
+FP4X4 = mybir.dt.float4_e2m1fn_x4
+ALU = mybir.AluOpType
+ACT = mybir.ActivationFunctionType
+
+P = 128
+SCALAR_RELU = 1
+CHUNKS = ((0, 256), (256, 128), (384, 128))
+
+
+def tile_moe_ogt_relu2_silu_kernel(
+    tc, x_words, x_scales, wg_words, wg_scales, w1_words, w1_scales, w2_words, w2_scales, gate, offs, pos1, pos2,
+    out_0, out_1, out_2,
+):
+    nc = tc.nc
+    with ExitStack() as ctx:
+        keep = ctx.enter_context(tc.tile_pool(name="keep", bufs=1))
+        ring = ctx.enter_context(tc.tile_pool(name="ring", bufs=3))
+        psum = ctx.enter_context(tc.psum_pool(name="psum", bufs=1))
+
+        def kept(shape, dtype, name):
+            return keep.tile(shape, dtype, name=name, align_bytes=64)
+
+        offs_sb = keep.tile([P, S // 16], U16, name="offs_sb")
+        pos1_sb = keep.tile([P, T // 16], U16, name="pos1_sb")
+        pos2_sb = keep.tile([P, T // 16], U16, name="pos2_sb")
+        xw = kept([P, T], U32, "xw")
+        xs = kept([P, T], U8, "xs")
+        w1s_raw = kept([P, H], U8, "w1s_raw")
+        w2s_raw = kept([P, N], U8, "w2s_raw")
+        wgs_raw = kept([P, N], U8, "wgs_raw")
+        for plane in (w1s_raw, w2s_raw):
+            nc.gpsimd.memset(plane[:].bitcast(I32), 0)
+
+        def load_words(dst, src):
+            nc.sync.dma_start(out=dst[:].bitcast(I32), in_=src.rearrange("p n d -> p (n d)").bitcast(I32))
+
+        def load_plane(dst, src):
+            for q in range(4):
+                rows = src[0, 4 * q : 4 * q + 4, :].bitcast(I32)
+                nc.sync.dma_start(out=dst[32 * q : 32 * q + 32, :].bitcast(I32), in_=rows.unsqueeze(0).to_broadcast([8, 4, N // 4]))
+
+        def load_planes(dst, src):
+            for q in range(4):
+                nc.sync.dma_start(out=dst[32 * q : 32 * q + 16, :].bitcast(I32), in_=src[:, 0, 4 * q : 4 * q + 4, :].bitcast(I32))
+
+        def staged(dtype, name):
+            return keep.tile([P, N], dtype, name=name, tag="staged", bufs=4, align_bytes=64)
+
+        w1_raw = [staged(U32, f"w1_raw{e}") for e in range(E)]
+        w2_raw = [staged(U32, f"w2_raw{e}") for e in range(E)]
+        wg_raw = kept([P, N], U16, "wg_raw")
+        g1 = staged(F32, "g1")
+        g2 = staged(F32, "g2")
+
+        nc.sync.dma_start(offs_sb[:], offs)
+        load_words(xw, x_words[0])
+        load_words(w1_raw[0], w1_words[0, 0])
+        load_plane(xs, x_scales)
+        load_planes(w1s_raw, w1_scales)
+        for e in range(1, E):
+            load_words(w1_raw[e], w1_words[e, 0])
+
+        def deal(copy, raw, dtype, name):
+            dealt = kept([P, 4, P], dtype, name)
+            copy(dealt[:].rearrange("p d m -> p m d"), raw[:].rearrange("p (m d) -> p m d", d=4))
+            return dealt
+
+        xg = [keep.tile([P, C], U32, name=f"xg{e}", tag="xg", bufs=2, align_bytes=64) for e in range(E)]
+        xgs = [keep.tile([P, C], U8, name=f"xgs{e}", tag="xgs", bufs=2, align_bytes=64) for e in range(E)]
+        hq = [kept([P, C], U32, f"hq{e}") for e in range(E)]
+        hs = [kept([P, C], U8, f"hs{e}") for e in range(E)]
+        y = [kept([P, S], F32, f"y{d}") for d in range(4)]
+        o = kept([P, 4, T], F32, "o")
+
+        def gather(e):
+            cols = offs_sb[:, e * C // 16 : (e + 1) * C // 16]
+            nc.vector.tensor_copy(xg[e][:], xw[:].indirect(cols))
+            nc.vector.tensor_copy(xgs[e][:], xs[:].indirect(cols))
+
+        def layer1(e, w1d, w1s):
+            hb = ring.tile([P, C, 4], BF16, name="hb", align_bytes=64)
+            for half in range(2):
+                cols = slice(half * P, (half + 1) * P)
+                bank = psum.tile([P, 4, P], F32, name="h_bank", bufs=3)
+                for d in range(4):
+                    nc.tensor.matmul_mx(
+                        out=bank[:, d, :], lhsT=w1d[:, d, :].bitcast(FP8X4), lhsT_scale=w1s[4 * e : P, d, :],
+                        rhs=xg[e][:, cols].bitcast(FP8X4), rhs_scale=xgs[e][:, cols], start=True, stop=True,
+                    )
+                r = ring.tile([P, P, 4], F32, name="relu", align_bytes=64)
+                if 2 * e + half < SCALAR_RELU:
+                    nc.scalar.activation(r[:], bank[:].rearrange("p d n -> p n d"), ACT.Relu)
+                else:
+                    nc.vector.tensor_scalar_max(r[:], bank[:].rearrange("p d n -> p n d"), 0.0)
+                nc.scalar.activation(hb[:, cols, :], r[:], ACT.Square)
+            return hb
+
+        def quantise_h(e, hb):
+            nc.vector.quantize_mx(out=hq[e][:].bitcast(FP8X4), scales=hs[e][:], in_=hb[:].rearrange("p n d -> p (n d)"))
+
+        def layer2(d, pair, w2d, w2s):
+            bank = psum.tile([P, 2, C], F32, name="y_bank", bufs=3)
+            for j in range(2):
+                e = 2 * pair + j
+                nc.tensor.matmul_mx(
+                    out=bank[:, j, :], lhsT=w2d[e][:, d, :].bitcast(FP8X4), lhsT_scale=w2s[4 * e : P, d, :],
+                    rhs=hq[e][:].bitcast(FP8X4), rhs_scale=hs[e][:], start=True, stop=True,
+                )
+            nc.scalar.copy(y[d][:, 2 * pair * C : 2 * (pair + 1) * C], bank[:].rearrange("p j n -> p (j n)"))
+
+        def output_gate():
+            wgd = deal(nc.scalar.copy, wg_raw, U16, "wgd")
+            wgs = deal(nc.vector.tensor_copy, wgs_raw, U8, "wgs")
+            for d in range(4):
+                bank = psum.tile([P, T], F32, name="z_bank", bufs=2)
+                nc.tensor.matmul_mx(
+                    out=bank[:], lhsT=wgd[:, d, :].bitcast(FP4X4), lhsT_scale=wgs[:, d, :],
+                    rhs=xw[:].bitcast(FP8X4), rhs_scale=xs[:], start=True, stop=True,
+                )
+                nc.scalar.activation(o[:, d, :], bank[:], ACT.Silu)
+
+        gather(0)
+        w1s = deal(nc.vector.tensor_copy, w1s_raw, U8, "w1s")
+        w1d = [deal(nc.scalar.copy, w1_raw[e], U32, f"w1d{e}") for e in range(E)]
+        for e in range(E):
+            load_words(w2_raw[e], w2_words[e, 0])
+        load_planes(w2s_raw, w2_scales)
+        nc.sync.dma_start(pos1_sb[:], pos1)
+        nc.sync.dma_start(pos2_sb[:], pos2)
+        nc.sync.dma_start(out=wg_raw[:].bitcast(I32), in_=wg_words[0].bitcast(I32))
+        load_plane(wgs_raw, wg_scales)
+        gather(1)
+        hb = {0: layer1(0, w1d[0], w1s)}
+        for e in range(E):
+            if e + 2 < E:
+                gather(e + 2)
+            if e + 1 < E:
+                hb[e + 1] = layer1(e + 1, w1d[e + 1], w1s)
+            quantise_h(e, hb[e])
+        w2s = deal(nc.vector.tensor_copy, w2s_raw, U8, "w2s")
+        w2d = [deal(nc.vector.tensor_copy, w2_raw[e], U32, f"w2d{e}") for e in range(E)]
+        nc.sync.dma_start(out=g1[:], in_=gate[0])
+        nc.sync.dma_start(out=g2[:], in_=gate[1])
+        for pair in range(2):
+            for d in range(4):
+                layer2(d, pair, w2d, w2s)
+        output_gate()
+
+        oq = kept([P, T], U32, "oq")
+        os_ = kept([P, T], U8, "oscale")
+        out_rows = out_0.rearrange("(p d) t -> p d t", d=4)
+        out_words = out_1[0].rearrange("p t d -> p (t d)").bitcast(I32)
+        res = kept([P, 4, T], F32, "res")
+
+        def combine(d, t0, n):
+            cols = slice(t0, t0 + n)
+            lcols = slice(t0 // 16, (t0 + n) // 16)
+            a = ring.tile([P, n], F32, name="a", align_bytes=64)
+            b = ring.tile([P, n], F32, name="b", align_bytes=64)
+            nc.scalar.activation(b[:], y[d][:].indirect(pos2_sb[:, lcols]), ACT.Copy)
+            nc.vector.tensor_tensor(a[:], y[d][:].indirect(pos1_sb[:, lcols]), g1[:, cols], ALU.mult)
+            nc.vector.tensor_tensor(b[:], b[:], g2[:, cols], ALU.mult)
+            nc.vector.tensor_tensor(a[:], a[:], b[:], ALU.add)
+            nc.vector.tensor_tensor(res[:, d, cols], a[:], o[:, d, cols], ALU.mult)
+            nc.sync.dma_start(out=out_rows[:, d, cols], in_=res[:, d, cols])
+
+        for d in range(3):
+            combine(d, 0, T)
+        for t0, n in CHUNKS:
+            cols = slice(t0, t0 + n)
+            combine(3, t0, n)
+            rb = kept([P, n, 4], BF16, f"rb{t0}")
+            nc.scalar.copy(rb[:].rearrange("p (c i) d -> p c d i", i=4), res[:, :, cols].rearrange("p d (c i) -> p c d i", i=4))
+            nc.vector.quantize_mx(out=oq[:, cols].bitcast(FP8X4), scales=os_[:, cols], in_=rb[:].rearrange("p t d -> p (t d)"))
+            nc.sync.dma_start(out=out_words[:, cols], in_=oq[:, cols].bitcast(I32))
+        for q in range(4):
+            nc.sync.dma_start(out=out_2[0, 4 * q : 4 * q + 4, :].bitcast(I32), in_=os_[32 * q : 32 * q + 4, :].bitcast(I32))

@@ -18,8 +18,11 @@ ALU = mybir.AluOpType
 ACT = mybir.ActivationFunctionType
 
 P = 128
-SCALAR_RELU = 1
-CHUNKS = ((0, 256), (256, 128), (384, 128))
+CHUNKS = ((0, 256, 2), (256, 128, 4), (384, 128, 4))
+SCALAR_RELU = (0,1,2,4,6)
+ROUND_ON_VECTOR = (384,)
+SCALAR_BOTH = ()
+GPSIMD_SQUARE = (0,2,4,6)
 
 
 def tile_moe_ogt_relu2_silu_kernel(
@@ -40,51 +43,55 @@ def tile_moe_ogt_relu2_silu_kernel(
         pos2_sb = keep.tile([P, T // 16], U16, name="pos2_sb")
         xw = kept([P, T], U32, "xw")
         xs = kept([P, T], U8, "xs")
-        w1s_raw = kept([P, H], U8, "w1s_raw")
-        w2s_raw = kept([P, N], U8, "w2s_raw")
-        wgs_raw = kept([P, N], U8, "wgs_raw")
-        for plane in (w1s_raw, w2s_raw):
+        w1s = keep.tile([P, H], U8, name="w1s", tag="reuse0", align_bytes=64)
+        w2s = kept([P, N], U8, "w2s")
+        wgs = kept([P, N], U8, "wgs")
+        for plane in (w1s, w2s):
             nc.gpsimd.memset(plane[:].bitcast(I32), 0)
 
         def load_words(dst, src):
             nc.sync.dma_start(out=dst[:].bitcast(I32), in_=src.rearrange("p n d -> p (n d)").bitcast(I32))
 
-        def load_plane(dst, src):
-            for q in range(4):
+        def load_experts(dst, src):
+            nc.sync.dma_start(out=dst[:].bitcast(I32), in_=src.rearrange("e p n d -> p e (n d)").bitcast(I32))
+
+        def load_plane(dst, src, quads=range(4)):
+            for q in quads:
                 rows = src[0, 4 * q : 4 * q + 4, :].bitcast(I32)
                 nc.sync.dma_start(out=dst[32 * q : 32 * q + 32, :].bitcast(I32), in_=rows.unsqueeze(0).to_broadcast([8, 4, N // 4]))
 
-        def load_planes(dst, src):
-            for q in range(4):
+        def load_planes(dst, src, quads=range(4)):
+            for q in quads:
                 nc.sync.dma_start(out=dst[32 * q : 32 * q + 16, :].bitcast(I32), in_=src[:, 0, 4 * q : 4 * q + 4, :].bitcast(I32))
 
-        def staged(dtype, name):
-            return keep.tile([P, N], dtype, name=name, tag="staged", bufs=4, align_bytes=64)
-
-        w1_raw = [staged(U32, f"w1_raw{e}") for e in range(E)]
-        w2_raw = [staged(U32, f"w2_raw{e}") for e in range(E)]
-        wg_raw = kept([P, N], U16, "wg_raw")
-        g1 = staged(F32, "g1")
-        g2 = staged(F32, "g2")
+        w1_pairs = [keep.tile([P, 2, H], U32, name=f"w1_pair{i}", tag=f"reuse{i + 1}", align_bytes=64) for i in range(2)]
+        w1 = [w1_pairs[e // 2][:, e % 2, :] for e in range(E)]
+        w2_pairs = [kept([P, 2, N], U32, f"w2_pair{i}") for i in range(2)]
+        w2 = [w2_pairs[e // 2][:, e % 2, :] for e in range(E)]
+        wg = kept([P, N], U16, "wg")
+        g = kept([P, 2, T], F32, "g")
 
         nc.sync.dma_start(offs_sb[:], offs)
         load_words(xw, x_words[0])
-        load_words(w1_raw[0], w1_words[0, 0])
         load_plane(xs, x_scales)
-        load_planes(w1s_raw, w1_scales)
-        for e in range(1, E):
-            load_words(w1_raw[e], w1_words[e, 0])
+        load_experts(w1_pairs[0], w1_words[0:2, 0])
+        load_experts(w1_pairs[1], w1_words[2:4, 0])
+        load_planes(w1s, w1_scales)
+        load_experts(w2_pairs[0], w2_words[0:2, 0])
+        load_planes(w2s, w2_scales)
+        load_experts(w2_pairs[1], w2_words[2:4, 0])
+        nc.sync.dma_start(out=wg[:].bitcast(I32), in_=wg_words[0].bitcast(I32))
+        load_plane(wgs, wg_scales)
+        nc.sync.dma_start(pos1_sb[:], pos1)
+        nc.sync.dma_start(pos2_sb[:], pos2)
+        nc.sync.dma_start(out=g[:], in_=gate.rearrange("r p t -> p r t"))
 
-        def deal(copy, raw, dtype, name):
-            dealt = kept([P, 4, P], dtype, name)
-            copy(dealt[:].rearrange("p d m -> p m d"), raw[:].rearrange("p (m d) -> p m d", d=4))
-            return dealt
-
-        xg = [keep.tile([P, C], U32, name=f"xg{e}", tag="xg", bufs=2, align_bytes=64) for e in range(E)]
-        xgs = [keep.tile([P, C], U8, name=f"xgs{e}", tag="xgs", bufs=2, align_bytes=64) for e in range(E)]
+        xg = [keep.tile([P, C], U32, name=f"xg{e}", tag=tag, align_bytes=64) for e, tag in enumerate(("xg0", "xg1", "reuse0", "xg0"))]
+        xgs = [keep.tile([P, C], U8, name=f"xgs{e}", tag=tag, align_bytes=64) for e, tag in enumerate(("xgs0", "xgs1", "reuse1", "reuse2"))]
         hq = [kept([P, C], U32, f"hq{e}") for e in range(E)]
         hs = [kept([P, C], U8, f"hs{e}") for e in range(E)]
-        y = [kept([P, S], F32, f"y{d}") for d in range(4)]
+        hb = [kept([P, C, 4], BF16, f"hb{e}") for e in range(E)]
+        y = [kept([P, S], F32, f"y{c}") for c in range(4)]
         o = kept([P, 4, T], F32, "o")
 
         def gather(e):
@@ -92,101 +99,116 @@ def tile_moe_ogt_relu2_silu_kernel(
             nc.vector.tensor_copy(xg[e][:], xw[:].indirect(cols))
             nc.vector.tensor_copy(xgs[e][:], xs[:].indirect(cols))
 
-        def layer1(e, w1d, w1s):
-            hb = ring.tile([P, C, 4], BF16, name="hb", align_bytes=64)
-            for half in range(2):
-                cols = slice(half * P, (half + 1) * P)
-                bank = psum.tile([P, 4, P], F32, name="h_bank", bufs=3)
-                for d in range(4):
-                    nc.tensor.matmul_mx(
-                        out=bank[:, d, :], lhsT=w1d[:, d, :].bitcast(FP8X4), lhsT_scale=w1s[4 * e : P, d, :],
-                        rhs=xg[e][:, cols].bitcast(FP8X4), rhs_scale=xgs[e][:, cols], start=True, stop=True,
-                    )
-                r = ring.tile([P, P, 4], F32, name="relu", align_bytes=64)
-                if 2 * e + half < SCALAR_RELU:
-                    nc.scalar.activation(r[:], bank[:].rearrange("p d n -> p n d"), ACT.Relu)
-                else:
-                    nc.vector.tensor_scalar_max(r[:], bank[:].rearrange("p d n -> p n d"), 0.0)
-                nc.scalar.activation(hb[:, cols, :], r[:], ACT.Square)
-            return hb
+        def deal(copy, raw, dtype, name, tag):
+            dealt = keep.tile([P, 4, P], dtype, name=name, tag=tag, align_bytes=64)
+            copy(dealt[:].rearrange("p d m -> p m d"), raw.rearrange("p (m d) -> p m d", d=4))
+            return dealt
 
-        def quantise_h(e, hb):
-            nc.vector.quantize_mx(out=hq[e][:].bitcast(FP8X4), scales=hs[e][:], in_=hb[:].rearrange("p n d -> p (n d)"))
-
-        def layer2(d, pair, w2d, w2s):
-            bank = psum.tile([P, 2, C], F32, name="y_bank", bufs=3)
-            for j in range(2):
-                e = 2 * pair + j
+        def layer1(u, w1d, w1sd):
+            e, cols = u // 2, slice(u % 2 * P, (u % 2 + 1) * P)
+            bank = psum.tile([P, 4, P], F32, name="z_bank", tag="a_bank", bufs=4)
+            for d in range(4):
                 nc.tensor.matmul_mx(
-                    out=bank[:, j, :], lhsT=w2d[e][:, d, :].bitcast(FP8X4), lhsT_scale=w2s[4 * e : P, d, :],
+                    out=bank[:, d, :], lhsT=w1d[e][:, d, :].bitcast(FP8X4), lhsT_scale=w1sd[4 * e : P, d, :],
+                    rhs=xg[e][:, cols].bitcast(FP8X4), rhs_scale=xgs[e][:, cols], start=True, stop=True,
+                )
+            r = ring.tile([P, P, 4], F32, name="relu", bufs=8, align_bytes=64)
+            if u in SCALAR_RELU:
+                nc.scalar.activation(r[:], bank[:].rearrange("p d n -> p n d"), ACT.Relu)
+            else:
+                nc.vector.tensor_scalar_max(r[:], bank[:].rearrange("p d n -> p n d"), 0.0)
+            if u in GPSIMD_SQUARE:
+                nc.gpsimd.tensor_tensor(hb[e][:, cols, :], r[:], r[:], ALU.mult)
+            else:
+                nc.scalar.activation(hb[e][:, cols, :], r[:], ACT.Square)
+
+        def quantise_h(e):
+            nc.vector.quantize_mx(out=hq[e][:].bitcast(FP8X4), scales=hs[e][:], in_=hb[e][:].rearrange("p n d -> p (n d)"))
+
+        def layer2(c, e0, ne, copy, w2d, w2sd):
+            bank = psum.tile([P, ne, C], F32, name="y_bank", tag="b_bank", bufs=4)
+            for j in range(ne):
+                e = e0 + j
+                nc.tensor.matmul_mx(
+                    out=bank[:, j, :], lhsT=w2d[e][:, c, :].bitcast(FP8X4), lhsT_scale=w2sd[4 * e : P, c, :],
                     rhs=hq[e][:].bitcast(FP8X4), rhs_scale=hs[e][:], start=True, stop=True,
                 )
-            nc.scalar.copy(y[d][:, 2 * pair * C : 2 * (pair + 1) * C], bank[:].rearrange("p j n -> p (j n)"))
+            copy(y[c][:, e0 * C : (e0 + ne) * C], bank[:].rearrange("p j n -> p (j n)"))
 
-        def output_gate():
-            wgd = deal(nc.scalar.copy, wg_raw, U16, "wgd")
-            wgs = deal(nc.vector.tensor_copy, wgs_raw, U8, "wgs")
-            for d in range(4):
-                bank = psum.tile([P, T], F32, name="z_bank", bufs=2)
-                nc.tensor.matmul_mx(
-                    out=bank[:], lhsT=wgd[:, d, :].bitcast(FP4X4), lhsT_scale=wgs[:, d, :],
-                    rhs=xw[:].bitcast(FP8X4), rhs_scale=xs[:], start=True, stop=True,
-                )
-                nc.scalar.activation(o[:, d, :], bank[:], ACT.Silu)
+        def output_gate(d, wgd, wgsd):
+            bank = psum.tile([P, T], F32, name="g_bank", tag="a_bank", bufs=4)
+            nc.tensor.matmul_mx(
+                out=bank[:], lhsT=wgd[:, d, :].bitcast(FP4X4), lhsT_scale=wgsd[:, d, :],
+                rhs=xw[:].bitcast(FP8X4), rhs_scale=xs[:], start=True, stop=True,
+            )
+            nc.scalar.activation(o[:, d, :], bank[:], ACT.Silu)
 
         gather(0)
-        w1s = deal(nc.vector.tensor_copy, w1s_raw, U8, "w1s")
-        w1d = [deal(nc.scalar.copy, w1_raw[e], U32, f"w1d{e}") for e in range(E)]
-        for e in range(E):
-            load_words(w2_raw[e], w2_words[e, 0])
-        load_planes(w2s_raw, w2_scales)
-        nc.sync.dma_start(pos1_sb[:], pos1)
-        nc.sync.dma_start(pos2_sb[:], pos2)
-        nc.sync.dma_start(out=wg_raw[:].bitcast(I32), in_=wg_words[0].bitcast(I32))
-        load_plane(wgs_raw, wg_scales)
+        w1sd = deal(nc.vector.tensor_copy, w1s[:], U8, "w1sd", "w1sd")
+        w1d = [deal(nc.scalar.copy, w1[e], U32, f"w1d{e}", f"w1d{e}") for e in range(E)]
         gather(1)
-        hb = {0: layer1(0, w1d[0], w1s)}
-        for e in range(E):
-            if e + 2 < E:
-                gather(e + 2)
-            if e + 1 < E:
-                hb[e + 1] = layer1(e + 1, w1d[e + 1], w1s)
-            quantise_h(e, hb[e])
-        w2s = deal(nc.vector.tensor_copy, w2s_raw, U8, "w2s")
-        w2d = [deal(nc.vector.tensor_copy, w2_raw[e], U32, f"w2d{e}") for e in range(E)]
-        nc.sync.dma_start(out=g1[:], in_=gate[0])
-        nc.sync.dma_start(out=g2[:], in_=gate[1])
-        for pair in range(2):
-            for d in range(4):
-                layer2(d, pair, w2d, w2s)
-        output_gate()
+        for u in range(2 * E):
+            layer1(u, w1d, w1sd)
+            if u % 2 == 1 and u // 2 + 2 < E:
+                gather(u // 2 + 2)
+            if u > 0 and u % 2 == 0:
+                quantise_h(u // 2 - 1)
+        quantise_h(E - 1)
+        w2sd = deal(nc.vector.tensor_copy, w2s[:], U8, "w2sd", "xgs1")
+        w2d = [deal(nc.vector.tensor_copy if e in (0,1,2,3) else nc.scalar.copy, w2[e], U32, f"w2d{e}", f"w1d{e}") for e in range(E)]
+        for c in range(4):
+            layer2(c, 0, 2, nc.vector.tensor_copy if c in () else nc.scalar.copy, w2d, w2sd)
+        wgd = deal(nc.scalar.copy, wg[:], U16, "wgd", "reuse0")
+        wgsd = deal(nc.vector.tensor_copy, wgs[:], U8, "wgsd", "w1sd")
 
         oq = kept([P, T], U32, "oq")
         os_ = kept([P, T], U8, "oscale")
+        res = kept([P, 4, T], F32, "res")
         out_rows = out_0.rearrange("(p d) t -> p d t", d=4)
         out_words = out_1[0].rearrange("p t d -> p (t d)").bitcast(I32)
-        res = kept([P, 4, T], F32, "res")
 
-        def combine(d, t0, n):
+        def fetch(t0, n, d0, nd):
             cols = slice(t0, t0 + n)
-            lcols = slice(t0 // 16, (t0 + n) // 16)
-            a = ring.tile([P, n], F32, name="a", align_bytes=64)
-            b = ring.tile([P, n], F32, name="b", align_bytes=64)
-            nc.scalar.activation(b[:], y[d][:].indirect(pos2_sb[:, lcols]), ACT.Copy)
-            nc.vector.tensor_tensor(a[:], y[d][:].indirect(pos1_sb[:, lcols]), g1[:, cols], ALU.mult)
-            nc.vector.tensor_tensor(b[:], b[:], g2[:, cols], ALU.mult)
-            nc.vector.tensor_tensor(a[:], a[:], b[:], ALU.add)
-            nc.vector.tensor_tensor(res[:, d, cols], a[:], o[:, d, cols], ALU.mult)
-            nc.sync.dma_start(out=out_rows[:, d, cols], in_=res[:, d, cols])
+            ab = keep.tile([P, 2, nd, n], F32, name="ab", bufs=4, align_bytes=64)
+            for j in range(nd):
+                for r, pos_sb in ((1, pos2_sb), (0, pos1_sb)):
+                    window = y[d0 + j][:].indirect(pos_sb[:, t0 // 16 : (t0 + n) // 16])
+                    if r == 1 or t0 in SCALAR_BOTH:
+                        nc.scalar.activation(ab[:, r, j, :], window, ACT.Copy)
+                    else:
+                        nc.vector.tensor_tensor(ab[:, r, j, :], window, g[:, r, cols], ALU.mult)
+            return ab
 
-        for d in range(3):
-            combine(d, 0, T)
-        for t0, n in CHUNKS:
+        def combine(ab, t0, n, d0, nd):
             cols = slice(t0, t0 + n)
-            combine(3, t0, n)
+            r0 = 0 if t0 in SCALAR_BOTH else 1
+            nc.vector.tensor_tensor(ab[:, r0:], ab[:, r0:], g[:, r0:, cols].unsqueeze(2).to_broadcast([P, 2 - r0, nd, n]), ALU.mult)
+            nc.vector.tensor_tensor(ab[:, 0], ab[:, 0], ab[:, 1], ALU.add)
+            nc.vector.tensor_tensor(res[:, d0 : d0 + nd, cols], ab[:, 0], o[:, d0 : d0 + nd, cols], ALU.mult)
+
+        def planes(t0, n):
+            cols = slice(t0, t0 + n)
+            nc.sync.dma_start(out=out_rows[:, :, cols], in_=res[:, :, cols])
             rb = kept([P, n, 4], BF16, f"rb{t0}")
-            nc.scalar.copy(rb[:].rearrange("p (c i) d -> p c d i", i=4), res[:, :, cols].rearrange("p d (c i) -> p c d i", i=4))
+            copy = nc.vector.tensor_copy if t0 in ROUND_ON_VECTOR else nc.scalar.copy
+            copy(rb[:].rearrange("p (c i) d -> p c d i", i=4), res[:, :, cols].rearrange("p d (c i) -> p c d i", i=4))
             nc.vector.quantize_mx(out=oq[:, cols].bitcast(FP8X4), scales=os_[:, cols], in_=rb[:].rearrange("p t d -> p (t d)"))
             nc.sync.dma_start(out=out_words[:, cols], in_=oq[:, cols].bitcast(I32))
+
+        for c in range(4):
+            layer2(c, 2, 2, nc.vector.tensor_copy if c in (0,) else nc.scalar.copy, w2d, w2sd)
+        steps = [(t0, n, d0, nd) for t0, n, nd in CHUNKS for d0 in range(0, 4, nd)]
+        fetched = []
+        for k in range(len(steps) + 1):
+            if k < len(steps):
+                fetched.append(fetch(*steps[k]))
+            if k >= 1:
+                t0, n, d0, nd = steps[k - 1]
+                if t0 == 0:
+                    for d in range(d0, d0 + nd):
+                        output_gate(d, wgd, wgsd)
+                combine(fetched[k - 1], t0, n, d0, nd)
+                if d0 + nd == 4:
+                    planes(t0, n)
         for q in range(4):
-            nc.sync.dma_start(out=out_2[0, 4 * q : 4 * q + 4, :].bitcast(I32), in_=os_[32 * q : 32 * q + 4, :].bitcast(I32))
+            (nc.scalar if q % 2 else nc.sync).dma_start(out=out_2[0, 4 * q : 4 * q + 4, :].bitcast(I32), in_=os_[32 * q : 32 * q + 4, :].bitcast(I32))

@@ -19,10 +19,10 @@ ACT = mybir.ActivationFunctionType
 
 P = 128
 CHUNKS = ((0, 256, 2), (256, 128, 4), (384, 128, 4))
-SCALAR_RELU = (0,1,2,4,6)
+SCALAR_RELU = (0,1,2)
 ROUND_ON_VECTOR = (384,)
 SCALAR_BOTH = ()
-GPSIMD_SQUARE = (0,2,4,6)
+GPSIMD_SQUARE = ()
 
 
 def tile_moe_ogt_relu2_silu_kernel(
@@ -100,8 +100,9 @@ def tile_moe_ogt_relu2_silu_kernel(
             nc.vector.tensor_copy(xgs[e][:], xs[:].indirect(cols))
 
         def deal(copy, raw, dtype, name, tag):
+            line = {U32: 4, U16: 8, U8: 16}[dtype]
             dealt = keep.tile([P, 4, P], dtype, name=name, tag=tag, align_bytes=64)
-            copy(dealt[:].rearrange("p d m -> p m d"), raw.rearrange("p (m d) -> p m d", d=4))
+            copy(dealt[:].rearrange("p d (c i) -> p c d i", i=line), raw.rearrange("p (c i d) -> p c d i", i=line, d=4))
             return dealt
 
         def layer1(u, w1d, w1sd):

from contextlib import ExitStack

import concourse.mybir as mybir

K, T, E, C, H, N = 512, 512, 4, 256, 512, 512
S = E * C
FLOPS = 2 * K * N * T + 2 * K * H * S + 2 * H * N * S

F32 = mybir.dt.float32
BF16 = mybir.dt.bfloat16
I32 = mybir.dt.int32
U32 = mybir.dt.uint32
U16 = mybir.dt.uint16
U8 = mybir.dt.uint8
FP8X4 = mybir.dt.float8_e4m3fn_x4
FP4X4 = mybir.dt.float4_e2m1fn_x4
ALU = mybir.AluOpType
ACT = mybir.ActivationFunctionType

P = 128
CHUNKS = ((0, 256, 2), (256, 128, 4), (384, 128, 4))
SCALAR_RELU = (0,1,2)
ROUND_ON_VECTOR = (384,)
SCALAR_BOTH = ()
GPSIMD_SQUARE = ()


def tile_moe_ogt_relu2_silu_kernel(
    tc, x_words, x_scales, wg_words, wg_scales, w1_words, w1_scales, w2_words, w2_scales, gate, offs, pos1, pos2,
    out_0, out_1, out_2,
):
    nc = tc.nc
    with ExitStack() as ctx:
        keep = ctx.enter_context(tc.tile_pool(name="keep", bufs=1))
        ring = ctx.enter_context(tc.tile_pool(name="ring", bufs=3))
        psum = ctx.enter_context(tc.psum_pool(name="psum", bufs=1))

        def kept(shape, dtype, name):
            return keep.tile(shape, dtype, name=name, align_bytes=64)

        offs_sb = keep.tile([P, S // 16], U16, name="offs_sb")
        pos1_sb = keep.tile([P, T // 16], U16, name="pos1_sb")
        pos2_sb = keep.tile([P, T // 16], U16, name="pos2_sb")
        xw = kept([P, T], U32, "xw")
        xs = kept([P, T], U8, "xs")
        w1s = keep.tile([P, H], U8, name="w1s", tag="reuse0", align_bytes=64)
        w2s = kept([P, N], U8, "w2s")
        wgs = kept([P, N], U8, "wgs")
        for plane in (w1s, w2s):
            nc.gpsimd.memset(plane[:].bitcast(I32), 0)

        def load_words(dst, src):
            nc.sync.dma_start(out=dst[:].bitcast(I32), in_=src.rearrange("p n d -> p (n d)").bitcast(I32))

        def load_experts(dst, src):
            nc.sync.dma_start(out=dst[:].bitcast(I32), in_=src.rearrange("e p n d -> p e (n d)").bitcast(I32))

        def load_plane(dst, src, quads=range(4)):
            for q in quads:
                rows = src[0, 4 * q : 4 * q + 4, :].bitcast(I32)
                nc.sync.dma_start(out=dst[32 * q : 32 * q + 32, :].bitcast(I32), in_=rows.unsqueeze(0).to_broadcast([8, 4, N // 4]))

        def load_planes(dst, src, quads=range(4)):
            for q in quads:
                nc.sync.dma_start(out=dst[32 * q : 32 * q + 16, :].bitcast(I32), in_=src[:, 0, 4 * q : 4 * q + 4, :].bitcast(I32))

        w1_pairs = [keep.tile([P, 2, H], U32, name=f"w1_pair{i}", tag=f"reuse{i + 1}", align_bytes=64) for i in range(2)]
        w1 = [w1_pairs[e // 2][:, e % 2, :] for e in range(E)]
        w2_pairs = [kept([P, 2, N], U32, f"w2_pair{i}") for i in range(2)]
        w2 = [w2_pairs[e // 2][:, e % 2, :] for e in range(E)]
        wg = kept([P, N], U16, "wg")
        g = kept([P, 2, T], F32, "g")

        nc.sync.dma_start(offs_sb[:], offs)
        load_words(xw, x_words[0])
        load_plane(xs, x_scales)
        load_experts(w1_pairs[0], w1_words[0:2, 0])
        load_experts(w1_pairs[1], w1_words[2:4, 0])
        load_planes(w1s, w1_scales)
        load_experts(w2_pairs[0], w2_words[0:2, 0])
        load_planes(w2s, w2_scales)
        load_experts(w2_pairs[1], w2_words[2:4, 0])
        nc.sync.dma_start(out=wg[:].bitcast(I32), in_=wg_words[0].bitcast(I32))
        load_plane(wgs, wg_scales)
        nc.sync.dma_start(pos1_sb[:], pos1)
        nc.sync.dma_start(pos2_sb[:], pos2)
        nc.sync.dma_start(out=g[:], in_=gate.rearrange("r p t -> p r t"))

        xg = [keep.tile([P, C], U32, name=f"xg{e}", tag=tag, align_bytes=64) for e, tag in enumerate(("xg0", "xg1", "reuse0", "xg0"))]
        xgs = [keep.tile([P, C], U8, name=f"xgs{e}", tag=tag, align_bytes=64) for e, tag in enumerate(("xgs0", "xgs1", "reuse1", "reuse2"))]
        hq = [kept([P, C], U32, f"hq{e}") for e in range(E)]
        hs = [kept([P, C], U8, f"hs{e}") for e in range(E)]
        hb = [kept([P, C, 4], BF16, f"hb{e}") for e in range(E)]
        y = [kept([P, S], F32, f"y{c}") for c in range(4)]
        o = kept([P, 4, T], F32, "o")

        def gather(e):
            cols = offs_sb[:, e * C // 16 : (e + 1) * C // 16]
            nc.vector.tensor_copy(xg[e][:], xw[:].indirect(cols))
            nc.vector.tensor_copy(xgs[e][:], xs[:].indirect(cols))

        def deal(copy, raw, dtype, name, tag):
            line = {U32: 4, U16: 8, U8: 16}[dtype]
            dealt = keep.tile([P, 4, P], dtype, name=name, tag=tag, align_bytes=64)
            copy(dealt[:].rearrange("p d (c i) -> p c d i", i=line), raw.rearrange("p (c i d) -> p c d i", i=line, d=4))
            return dealt

        def layer1(u, w1d, w1sd):
            e, cols = u // 2, slice(u % 2 * P, (u % 2 + 1) * P)
            bank = psum.tile([P, 4, P], F32, name="z_bank", tag="a_bank", bufs=4)
            for d in range(4):
                nc.tensor.matmul_mx(
                    out=bank[:, d, :], lhsT=w1d[e][:, d, :].bitcast(FP8X4), lhsT_scale=w1sd[4 * e : P, d, :],
                    rhs=xg[e][:, cols].bitcast(FP8X4), rhs_scale=xgs[e][:, cols], start=True, stop=True,
                )
            r = ring.tile([P, P, 4], F32, name="relu", bufs=8, align_bytes=64)
            if u in SCALAR_RELU:
                nc.scalar.activation(r[:], bank[:].rearrange("p d n -> p n d"), ACT.Relu)
            else:
                nc.vector.tensor_scalar_max(r[:], bank[:].rearrange("p d n -> p n d"), 0.0)
            if u in GPSIMD_SQUARE:
                nc.gpsimd.tensor_tensor(hb[e][:, cols, :], r[:], r[:], ALU.mult)
            else:
                nc.scalar.activation(hb[e][:, cols, :], r[:], ACT.Square)

        def quantise_h(e):
            nc.vector.quantize_mx(out=hq[e][:].bitcast(FP8X4), scales=hs[e][:], in_=hb[e][:].rearrange("p n d -> p (n d)"))

        def layer2(c, e0, ne, copy, w2d, w2sd):
            bank = psum.tile([P, ne, C], F32, name="y_bank", tag="b_bank", bufs=4)
            for j in range(ne):
                e = e0 + j
                nc.tensor.matmul_mx(
                    out=bank[:, j, :], lhsT=w2d[e][:, c, :].bitcast(FP8X4), lhsT_scale=w2sd[4 * e : P, c, :],
                    rhs=hq[e][:].bitcast(FP8X4), rhs_scale=hs[e][:], start=True, stop=True,
                )
            copy(y[c][:, e0 * C : (e0 + ne) * C], bank[:].rearrange("p j n -> p (j n)"))

        def output_gate(d, wgd, wgsd):
            bank = psum.tile([P, T], F32, name="g_bank", tag="a_bank", bufs=4)
            nc.tensor.matmul_mx(
                out=bank[:], lhsT=wgd[:, d, :].bitcast(FP4X4), lhsT_scale=wgsd[:, d, :],
                rhs=xw[:].bitcast(FP8X4), rhs_scale=xs[:], start=True, stop=True,
            )
            nc.scalar.activation(o[:, d, :], bank[:], ACT.Silu)

        gather(0)
        w1sd = deal(nc.vector.tensor_copy, w1s[:], U8, "w1sd", "w1sd")
        w1d = [deal(nc.scalar.copy, w1[e], U32, f"w1d{e}", f"w1d{e}") for e in range(E)]
        gather(1)
        for u in range(2 * E):
            layer1(u, w1d, w1sd)
            if u % 2 == 1 and u // 2 + 2 < E:
                gather(u // 2 + 2)
            if u > 0 and u % 2 == 0:
                quantise_h(u // 2 - 1)
        quantise_h(E - 1)
        w2sd = deal(nc.vector.tensor_copy, w2s[:], U8, "w2sd", "xgs1")
        w2d = [deal(nc.vector.tensor_copy if e in (0,1,2,3) else nc.scalar.copy, w2[e], U32, f"w2d{e}", f"w1d{e}") for e in range(E)]
        for c in range(4):
            layer2(c, 0, 2, nc.vector.tensor_copy if c in () else nc.scalar.copy, w2d, w2sd)
        wgd = deal(nc.scalar.copy, wg[:], U16, "wgd", "reuse0")
        wgsd = deal(nc.vector.tensor_copy, wgs[:], U8, "wgsd", "w1sd")

        oq = kept([P, T], U32, "oq")
        os_ = kept([P, T], U8, "oscale")
        res = kept([P, 4, T], F32, "res")
        out_rows = out_0.rearrange("(p d) t -> p d t", d=4)
        out_words = out_1[0].rearrange("p t d -> p (t d)").bitcast(I32)

        def fetch(t0, n, d0, nd):
            cols = slice(t0, t0 + n)
            ab = keep.tile([P, 2, nd, n], F32, name="ab", bufs=4, align_bytes=64)
            for j in range(nd):
                for r, pos_sb in ((1, pos2_sb), (0, pos1_sb)):
                    window = y[d0 + j][:].indirect(pos_sb[:, t0 // 16 : (t0 + n) // 16])
                    if r == 1 or t0 in SCALAR_BOTH:
                        nc.scalar.activation(ab[:, r, j, :], window, ACT.Copy)
                    else:
                        nc.vector.tensor_tensor(ab[:, r, j, :], window, g[:, r, cols], ALU.mult)
            return ab

        def combine(ab, t0, n, d0, nd):
            cols = slice(t0, t0 + n)
            r0 = 0 if t0 in SCALAR_BOTH else 1
            nc.vector.tensor_tensor(ab[:, r0:], ab[:, r0:], g[:, r0:, cols].unsqueeze(2).to_broadcast([P, 2 - r0, nd, n]), ALU.mult)
            nc.vector.tensor_tensor(ab[:, 0], ab[:, 0], ab[:, 1], ALU.add)
            nc.vector.tensor_tensor(res[:, d0 : d0 + nd, cols], ab[:, 0], o[:, d0 : d0 + nd, cols], ALU.mult)

        def planes(t0, n):
            cols = slice(t0, t0 + n)
            nc.sync.dma_start(out=out_rows[:, :, cols], in_=res[:, :, cols])
            rb = kept([P, n, 4], BF16, f"rb{t0}")
            copy = nc.vector.tensor_copy if t0 in ROUND_ON_VECTOR else nc.scalar.copy
            copy(rb[:].rearrange("p (c i) d -> p c d i", i=4), res[:, :, cols].rearrange("p d (c i) -> p c d i", i=4))
            nc.vector.quantize_mx(out=oq[:, cols].bitcast(FP8X4), scales=os_[:, cols], in_=rb[:].rearrange("p t d -> p (t d)"))
            nc.sync.dma_start(out=out_words[:, cols], in_=oq[:, cols].bitcast(I32))

        for c in range(4):
            layer2(c, 2, 2, nc.vector.tensor_copy if c in (0,) else nc.scalar.copy, w2d, w2sd)
        steps = [(t0, n, d0, nd) for t0, n, nd in CHUNKS for d0 in range(0, 4, nd)]
        fetched = []
        for k in range(len(steps) + 1):
            if k < len(steps):
                fetched.append(fetch(*steps[k]))
            if k >= 1:
                t0, n, d0, nd = steps[k - 1]
                if t0 == 0:
                    for d in range(d0, d0 + nd):
                        output_gate(d, wgd, wgsd)
                combine(fetched[k - 1], t0, n, d0, nd)
                if d0 + nd == 4:
                    planes(t0, n)
        for q in range(4):
            (nc.scalar if q % 2 else nc.sync).dma_start(out=out_2[0, 4 * q : 4 * q + 4, :].bitcast(I32), in_=os_[32 * q : 32 * q + 4, :].bitcast(I32))
